import numpy as np
import ml_dtypes


def mxq(x, axis, fmt="e4m3"):
    dtype, down = {"e4m3": (ml_dtypes.float8_e4m3fn, 7), "e5m2": (ml_dtypes.float8_e5m2, 14)}[fmt]
    v = np.moveaxis(np.asarray(x, np.float32).astype(ml_dtypes.bfloat16).astype(np.float64), axis, -1)
    blocks = v.reshape(v.shape[:-1] + (-1, 32))
    amax = np.abs(blocks).max(-1, keepdims=True)
    byte = np.maximum(np.where(amax > 0, np.frexp(amax)[1] - 1 + 127, 0) - down, 1)
    scale = np.exp2(byte - 127.0)
    codes = (blocks / scale).astype(np.float32).astype(dtype).astype(np.float64)
    return np.moveaxis((codes * scale).reshape(v.shape), -1, axis)


WIDE = False


def mx_kscale(k):
    if not WIDE:
        return np.ones(k)
    levels = np.array([24, -24, 12, -12, 0])
    if k % 512:
        return np.exp2(np.random.permutation(np.resize(levels, k // 32))).repeat(32)
    a = np.empty((k // 512, 16))
    for p in range(k // 512):
        a[p, :8] = np.random.permutation(np.resize(levels, 8))
        for g in range(8):
            far = levels[np.abs(levels - a[p, g]) >= 10]
            a[p, g + 8] = far[np.random.randint(len(far))]
    return np.exp2(a.ravel()).repeat(32)


def f64(x):
    return np.asarray(x).astype(np.float64)


def striped(idx):
    return np.tile(idx.reshape(-1, 16).T, (8, 1)).astype(np.uint16)


def unstriped(offs):
    return offs[:16].T.reshape(-1).astype(np.int64)


E2M1 = np.array([0.0, 0.5, 1.0, 1.5, 2.0, 3.0, 4.0, 6.0, -0.0, -0.5, -1.0, -1.5, -2.0, -3.0, -4.0, -6.0])


def pack_weight(w, fmt):
    k, n = w.shape
    w = f64(np.asarray(w, np.float32).astype(ml_dtypes.bfloat16)).reshape(k // 32, 32, n)
    amax = np.abs(w).max(1)
    if fmt == "e4m3":
        byte = np.frexp(amax)[1] - 1 + 127 - 7
    else:
        mant, ex = np.frexp(amax / 6.0)
        byte = np.where(mant > 0.5, ex, ex - 1) + 127
    byte = np.clip(np.where(amax > 0, byte, 1), 1, 254)
    scaled = (w * np.exp2(127.0 - byte)[:, None, :]).reshape(k, n).astype(np.float32)
    by_word = np.ascontiguousarray(scaled.reshape(k // 512, 128, 4, n).transpose(0, 1, 3, 2))
    if fmt == "e4m3":
        words = by_word.astype(ml_dtypes.float8_e4m3fn).view(np.uint8)
    else:
        c = by_word.astype(ml_dtypes.float4_e2m1fn).view(np.uint8) & 0xF
        words = (c[..., 0::2] | (c[..., 1::2] << 4)).reshape(k // 512, 128, 2 * n)
    return np.ascontiguousarray(words), np.ascontiguousarray(byte.astype(np.uint8).reshape(k // 512, 16, n))


def unpack_weight(words, scales, fmt):
    g, _, n = scales.shape
    words = np.ascontiguousarray(words).reshape(g, 128, n, -1)
    if fmt == "e4m3":
        vals = words.view(ml_dtypes.float8_e4m3fn).astype(np.float64)
    else:
        nib = np.empty((g, 128, n, 4), np.uint8)
        nib[..., 0::2] = words & 0xF
        nib[..., 1::2] = words >> 4
        vals = E2M1[nib]
    vals = vals * np.repeat(np.exp2(scales.astype(np.float64) - 127.0), 8, axis=1)[..., None]
    return vals.transpose(0, 1, 3, 2).reshape(g * 512, n)


def pack_table4(v):
    words, scales = pack_weight(v, "e2m1")
    g, t = words.shape[0] // 2, v.shape[1]
    return np.ascontiguousarray(words.reshape(g, 2, 128, t, 2).transpose(0, 2, 3, 1, 4).reshape(g, 128, t, 4)), scales


def unpack_table4(words, scales):
    g, _, t, _ = words.shape
    return unpack_weight(words.reshape(g, 128, t, 2, 2).transpose(0, 3, 1, 2, 4).reshape(2 * g, 128, 2 * t), scales, "e2m1")


def gelu(f):
    return 0.5 * f * (1.0 + np.tanh(np.sqrt(2.0 / np.pi) * (f + 0.044715 * f**3)))


K, L, R, N, T, J = 512, 1024, 1024, 512, 4096, 1024


def setup_inputs():
    n = np.random.standard_normal
    s = mx_kscale(K)[:, None]
    s2 = mx_kscale(L)[:, None]
    u = mx_kscale(R)[:, None]
    en = n((R, N)) / np.sqrt(R) / u
    p_tab = pack_weight(n((K, T)) * s, "e4m3")
    p_tab2 = pack_table4(n((L, T)) * s2)
    p_en8 = pack_weight(en[:512], "e4m3")
    p_en4 = pack_weight(en[512:], "e2m1")
    return {
        "tab_words": p_tab[0],
        "tab_scales": p_tab[1],
        "tab2_words": p_tab2[0],
        "tab2_scales": p_tab2[1],
        "wa": (n((K, R)) / np.sqrt(K) / s * u.T).astype(np.float32),
        "wb": (n((L, R)) / np.sqrt(L) / s2 * u.T).astype(np.float32),
        "en8_words": p_en8[0],
        "en8_scales": p_en8[1],
        "en4_words": p_en4[0],
        "en4_scales": p_en4[1],
        "b": (0.3 * n(N)).astype(np.float32),
        "offs": striped(np.random.permutation(T)[:J]),
        "offs2": striped(np.random.permutation(T)[:J]),
    }


def reference(tab_words, tab_scales, tab2_words, tab2_scales, wa, wb, en8_words, en8_scales, en4_words, en4_scales, b, offs, offs2):
    idx = unstriped(offs)
    idx2 = unstriped(offs2)
    tab_ = unpack_weight(tab_words, tab_scales, "e4m3")[:, idx]
    tab2_ = unpack_table4(tab2_words, tab2_scales)[:, idx2]
    wa_ = mxq(f64(wa), 0, "e4m3")
    wb_ = mxq(f64(wb), 0, "e4m3")
    ha = wa_.T @ tab_
    hb = wb_.T @ tab2_
    h = np.abs(ha - hb)
    h_ = mxq(h, 0, "e4m3")
    en8_ = unpack_weight(en8_words, en8_scales, "e4m3")
    en4_ = unpack_weight(en4_words, en4_scales, "e2m1")
    y = en8_.T @ h_[:512] + en4_.T @ h_[512:]
    return gelu(y + f64(b)[:, None])

@@ -1,0 +1,229 @@
+from contextlib import ExitStack
+
+import concourse.mybir as mybir
+
+K, L, R, N, T, J = 512, 1024, 1024, 512, 4096, 1024
+FLOPS = 2 * J * (K * R + L * R + R * N)
+
+F32 = mybir.dt.float32
+BF16 = mybir.dt.bfloat16
+I32 = mybir.dt.int32
+U32 = mybir.dt.uint32
+U16 = mybir.dt.uint16
+U8 = mybir.dt.uint8
+FP8X4 = mybir.dt.float8_e4m3fn_x4
+FP4X4 = mybir.dt.float4_e2m1fn_x4
+ACT = mybir.ActivationFunctionType
+ALU = mybir.AluOpType
+
+P = 128
+PACK = 4
+KP = P * PACK
+JS = 128
+BANKS = J // JS
+HALF = J // 2
+
+
+def tile_list_kg_absd_mix_gelu_kernel(
+    tc, tab_words, tab_scales, tab2_words, tab2_scales, wa, wb, en8_words, en8_scales, en4_words, en4_scales, b, offs, offs2, out
+):
+    nc = tc.nc
+    with ExitStack() as ctx:
+        keep = ctx.enter_context(tc.tile_pool(name="keep", bufs=1))
+        ring = ctx.enter_context(tc.tile_pool(name="ring", bufs=4))
+        psum = ctx.enter_context(tc.psum_pool(name="psum", bufs=1))
+
+        list1 = keep.tile([P, J // 16], U16, name="list1")
+        list2 = keep.tile([P, J // 16], U16, name="list2")
+        words2 = keep.tile([P, T], U32, name="words2", align_bytes=64)
+        scales1 = keep.tile([P, T], U8, name="scales1", align_bytes=64)
+        scales2 = keep.tile([P, T], U8, name="scales2", tag="scales2", align_bytes=64)
+        warm = keep.tile([P, 2], F32, name="warm")
+
+        nc.vector.memset(scales2[:].bitcast(I32), 0)
+        nc.gpsimd.memset(scales1[:].bitcast(I32), 0)
+        nc.vector.memset(warm[:, 0:1], 0.0)
+        nc.scalar.activation(warm[:, 1:2], warm[:, 0:1], ACT.Gelu_apprx_tanh)
+
+        def load_piece(kind, blk):
+            w, k0 = {"a": (wa, 0), "b0": (wb, 0), "b1": (wb, KP)}[kind]
+            raw[kind, blk] = keep.tile([P, PACK, KP], F32, name="raw_%s_%d" % (kind, blk), tag="raw_" + kind)
+            rows = w[k0 : k0 + KP, blk * KP : (blk + 1) * KP].rearrange("(p j) c -> p j c", j=PACK)
+            nc.sync.dma_start(raw[kind, blk][:], rows)
+
+        def load_words(tile, words, c0, c1):
+            rows = words[0].rearrange("p t i -> p (t i)").bitcast(I32)
+            nc.sync.dma_start(tile[:, c0:c1].bitcast(I32), rows[:, c0:c1])
+
+        raw = {}
+        nc.sync.dma_start(list2[:], offs2)
+        load_words(words2, tab2_words, 0, T // 2)
+        nc.sync.dma_start(list1[:], offs)
+        for r in range(4):
+            nc.sync.dma_start(scales2[r:P:16, :].bitcast(I32), tab2_scales[:, r:16:4, :].bitcast(I32).rearrange("a q t -> q a t"))
+        load_words(words2, tab2_words, T // 2, T)
+        load_piece("b0", 0)
+        load_piece("b1", 0)
+        for q in range(4):
+            nc.sync.dma_start(scales1[32 * q + 8 : 32 * q + 12, :].bitcast(I32), tab_scales[0, 4 * q : 4 * q + 4, :].bitcast(I32))
+        load_piece("a", 0)
+
+        w_codes, w_scales, grouped = {}, {}, {}
+
+        def cast(key, engine, t0, t1):
+            sign = -1.0 if key[0] == "a" else 1.0
+            name = "grp_%s_%d_%d" % (key[0], key[1], t0)
+            g = keep.tile([P, (t1 - t0) * KP], BF16, name=name, tag=name, align_bytes=64)
+            dst = g[:].rearrange("p (t m j) -> p m t j", j=PACK, m=P)
+            src = raw[key][:].rearrange("p j (m t) -> p m t j", t=PACK)[:, :, t0:t1, :]
+            if engine == "scalar":
+                nc.scalar.activation(dst, src, ACT.Copy, scale=sign)
+            elif sign < 0:
+                nc.vector.tensor_scalar(dst, src, sign, None, ALU.mult)
+            else:
+                nc.vector.tensor_copy(dst, src)
+            grouped[key, t0] = (g, t1)
+
+        def quantise(key, t0):
+            if key not in w_codes:
+                w_codes[key] = keep.tile([P, KP], U32, name="wc_%s_%d" % key, align_bytes=64)
+                w_scales[key] = keep.tile([P, KP], U8, name="ws_%s_%d" % key, align_bytes=64)
+            g, t1 = grouped[key, t0]
+            cols = slice(t0 * P, t1 * P)
+            nc.vector.quantize_mx(w_codes[key][:, cols].bitcast(FP8X4), w_scales[key][:, cols], g[:])
+
+        pair2 = keep.tile([P, J], U32, name="pair2", align_bytes=64)
+        picked2 = keep.tile([P, 2 * J], U16, name="picked2", align_bytes=64)
+        picked2_s = [keep.tile([P, J], U8, name="picked2_s%d" % a, align_bytes=64) for a in range(2)]
+        picked1 = [keep.tile([P, HALF], U32, name="picked1_%d" % h, align_bytes=64) for h in range(2)]
+        picked1_s = keep.tile([P, J], U8, name="picked1_s", align_bytes=64)
+
+        def moving(kind, s):
+            cols = slice(s * JS, (s + 1) * JS)
+            if kind == "a":
+                half, c0 = divmod(s * JS, HALF)
+                return picked1[half][:, c0 : c0 + JS].bitcast(FP8X4), picked1_s[8:P, cols]
+            a = int(kind[1])
+            return picked2[:, a * J + s * JS : a * J + (s + 1) * JS].bitcast(FP4X4), picked2_s[a][:, cols]
+
+        acc = {}
+
+        def stage1(kind, blk, s):
+            if kind == "b0":
+                acc[blk, s] = psum.tile([P, PACK * JS], F32, name="acc", tag="bank%d" % s)
+            rhs, rhs_s = moving(kind, s)
+            for t in range(PACK):
+                cols = slice(t * P, (t + 1) * P)
+                nc.tensor.matmul_mx(
+                    acc[blk, s][:, t * JS : (t + 1) * JS],
+                    lhsT=w_codes[kind, blk][:, cols].bitcast(FP8X4),
+                    lhsT_scale=w_scales[kind, blk][:, cols],
+                    rhs=rhs,
+                    rhs_scale=rhs_s,
+                    start=(kind == "b0" and t == 0),
+                    stop=(kind == "a" and t == PACK - 1),
+                )
+
+        h_codes = {(blk, hf): keep.tile([P, HALF], U32, name="hc_%d_%d" % (blk, hf), align_bytes=64) for blk in range(2) for hf in range(2)}
+        h_scales = {(blk, hf): keep.tile([P, HALF], U8, name="hs_%d_%d" % (blk, hf), align_bytes=64) for blk in range(2) for hf in range(2)}
+
+        h_tiles = {}
+
+        def join(blk, s):
+            group = 4 if blk == 0 else 1
+            g, i = divmod(s, group)
+            if i == 0:
+                h_tiles[blk, g] = keep.tile([P, group * JS * PACK], BF16, name="h_%d_%d" % (blk, g), align_bytes=64)
+            h = h_tiles[blk, g]
+            nc.scalar.activation(
+                h[:, i * JS * PACK : (i + 1) * JS * PACK].rearrange("p (j t) -> p j t", t=PACK),
+                acc[blk, s][:].rearrange("p (t j) -> p j t", t=PACK),
+                ACT.Abs,
+            )
+            if blk == 1:
+                quantise_h(blk, g)
+
+        def quantise_h(blk, g):
+            group = 4 if blk == 0 else 1
+            hf, c0 = divmod(g * group * JS, HALF)
+            cols = slice(c0, c0 + group * JS)
+            nc.vector.quantize_mx(h_codes[blk, hf][:, cols].bitcast(FP8X4), h_scales[blk, hf][:, cols], h_tiles[blk, g][:])
+
+        def stage2(hf):
+            for q in range(N // P):
+                y = psum.tile([P, HALF], F32, name="y", tag="bank%d" % (hf * 4 + q))
+                cols = slice(q * P, (q + 1) * P)
+                nc.tensor.matmul_mx(
+                    y[:], lhsT=en8[:, 4 * q * P : 4 * (q + 1) * P].bitcast(FP8X4), lhsT_scale=en8_s[:, cols],
+                    rhs=h_codes[0, hf][:].bitcast(FP8X4), rhs_scale=h_scales[0, hf][:], start=True, stop=False,
+                )
+                nc.tensor.matmul_mx(
+                    y[:], lhsT=en4[:, 2 * q * P : 2 * (q + 1) * P].bitcast(FP4X4), lhsT_scale=en4_s[:, cols],
+                    rhs=h_codes[1, hf][:].bitcast(FP8X4), rhs_scale=h_scales[1, hf][:], start=False, stop=True,
+                )
+                res = ring.tile([P, HALF], F32, name="res", bufs=8)
+                nc.scalar.activation(res[:], y[:], ACT.Gelu_apprx_tanh, bias=bias[:, q : q + 1])
+                nc.sync.dma_start(out[cols, hf * HALF : (hf + 1) * HALF], res[:])
+
+        nc.vector.memset(picked2_s[1][:].bitcast(I32), 0)
+        nc.vector.tensor_copy(picked2_s[0][:], scales2[:].indirect(list2[:]))
+        nc.sync.dma_start(picked2_s[1][0:100, :].bitcast(I32), picked2_s[0][16:116, :].bitcast(I32))
+        words1 = keep.tile([P, T], U32, name="words1", tag="scales2", align_bytes=64)
+        load_words(words1, tab_words, 0, T)
+        nc.vector.tensor_copy(pair2[:], words2[:].indirect(list2[:]))
+        nc.vector.tensor_copy(
+            picked2[:].rearrange("p (d j) -> p d j", d=2), pair2[:].bitcast(U16).rearrange("p (j d) -> p d j", d=2)
+        )
+        cast(("b0", 0), "scalar", 0, 4)
+        load_piece("b0", 1)
+        quantise(("b0", 0), 0)
+        cast(("b1", 0), "scalar", 0, 4)
+        load_piece("b1", 1)
+        cast(("a", 0), "scalar", 0, 4)
+        load_piece("a", 1)
+        quantise(("b1", 0), 0)
+        nc.vector.tensor_copy(picked1_s[:], scales1[:].indirect(list1[:]))
+        quantise(("a", 0), 0)
+        en = keep.tile([P, 8 * N], U8, name="en", tag="grp_a_0_0", align_bytes=64)
+        en8, en4, en8_s, en4_s = en[:, 0 : 4 * N], en[:, 4 * N : 6 * N], en[:, 6 * N : 7 * N], en[:, 7 * N : 8 * N]
+        nc.sync.dma_start(en8.bitcast(I32), en8_words[0].rearrange("p n i -> p (n i)").bitcast(I32))
+        nc.sync.dma_start(en4.bitcast(I32), en4_words[0].bitcast(I32))
+        nc.vector.memset(en[:, 6 * N : 8 * N].bitcast(I32), 0)
+        for q in range(4):
+            nc.sync.dma_start(en8_s[32 * q : 32 * q + 4, :].bitcast(I32), en8_scales[0, 4 * q : 4 * q + 4, :].bitcast(I32))
+            nc.sync.dma_start(en4_s[32 * q : 32 * q + 4, :].bitcast(I32), en4_scales[0, 4 * q : 4 * q + 4, :].bitcast(I32))
+        for s in range(BANKS):
+            stage1("b0", 0, s)
+        for s in range(BANKS):
+            stage1("b1", 0, s)
+        for hf in range(2):
+            nc.vector.tensor_copy(picked1[hf][:], words1[:].indirect(list1[:, hf * 32 : (hf + 1) * 32]))
+        cast(("b0", 1), "vector", 0, 4)
+        quantise(("b0", 1), 0)
+        bias = keep.tile([P, N // P], F32, name="bias", tag="grp_b0_1_0", align_bytes=64)
+        with nc.allow_non_contiguous_dma(reason="one bias value to a partition"):
+            nc.sync.dma_start(bias[:], b.rearrange("(c p) -> p c", p=P))
+        for s in range(BANKS):
+            stage1("a", 0, s)
+            join(0, s)
+        cast(("b1", 1), "vector", 0, 4)
+        quantise(("b1", 1), 0)
+        cast(("a", 1), "vector", 2, 4)
+        cast(("a", 1), "scalar", 0, 2)
+        quantise(("a", 1), 2)
+        quantise(("a", 1), 0)
+        for hf in range(2):
+            quantise_h(0, hf)
+        for s in range(BANKS):
+            stage1("b0", 1, s)
+        for s in range(4):
+            stage1("b1", 1, s)
+        for s in range(4):
+            stage1("a", 1, s)
+            join(1, s)
+        for s in range(4, BANKS):
+            stage1("b1", 1, s)
+            stage1("a", 1, s)
+            join(1, s)
+        for hf in range(2):
+            stage2(hf)

@@ -35,7 +35,7 @@ def tile_list_kg_absd_mix_gelu_kernel(
 
         list1 = keep.tile([P, J // 16], U16, name="list1")
         list2 = keep.tile([P, J // 16], U16, name="list2")
-        words2 = keep.tile([P, T], U32, name="words2", align_bytes=64)
+        words2 = keep.tile([P, T], U32, name="words2", tag="words2", align_bytes=64)
         scales1 = keep.tile([P, T], U8, name="scales1", align_bytes=64)
         scales2 = keep.tile([P, T], U8, name="scales2", tag="scales2", align_bytes=64)
         warm = keep.tile([P, 2], F32, name="warm")
@@ -47,7 +47,8 @@ def tile_list_kg_absd_mix_gelu_kernel(
 
         def load_piece(kind, blk):
             w, k0 = {"a": (wa, 0), "b0": (wb, 0), "b1": (wb, KP)}[kind]
-            raw[kind, blk] = keep.tile([P, PACK, KP], F32, name="raw_%s_%d" % (kind, blk), tag="raw_" + kind)
+            tag = "words2" if kind == "a" else "raw_" + kind
+            raw[kind, blk] = keep.tile([P, PACK, KP], F32, name="raw_%s_%d" % (kind, blk), tag=tag, align_bytes=64)
             rows = w[k0 : k0 + KP, blk * KP : (blk + 1) * KP].rearrange("(p j) c -> p j c", j=PACK)
             nc.sync.dma_start(raw[kind, blk][:], rows)
 
@@ -66,7 +67,6 @@ def tile_list_kg_absd_mix_gelu_kernel(
         load_piece("b1", 0)
         for q in range(4):
             nc.sync.dma_start(scales1[32 * q + 8 : 32 * q + 12, :].bitcast(I32), tab_scales[0, 4 * q : 4 * q + 4, :].bitcast(I32))
-        load_piece("a", 0)
 
         w_codes, w_scales, grouped = {}, {}, {}
 
@@ -74,8 +74,8 @@ def tile_list_kg_absd_mix_gelu_kernel(
             sign = -1.0 if key[0] == "a" else 1.0
             name = "grp_%s_%d_%d" % (key[0], key[1], t0)
             g = keep.tile([P, (t1 - t0) * KP], BF16, name=name, tag=name, align_bytes=64)
-            dst = g[:].rearrange("p (t m j) -> p m t j", j=PACK, m=P)
-            src = raw[key][:].rearrange("p j (m t) -> p m t j", t=PACK)[:, :, t0:t1, :]
+            dst = g[:].rearrange("p (t m j) -> p m j t", j=PACK, m=P)
+            src = raw[key][:].rearrange("p j (m t) -> p m j t", t=PACK)[:, :, :, t0:t1]
             if engine == "scalar":
                 nc.scalar.activation(dst, src, ACT.Copy, scale=sign)
             elif sign < 0:
@@ -95,14 +95,13 @@ def tile_list_kg_absd_mix_gelu_kernel(
         pair2 = keep.tile([P, J], U32, name="pair2", align_bytes=64)
         picked2 = keep.tile([P, 2 * J], U16, name="picked2", align_bytes=64)
         picked2_s = [keep.tile([P, J], U8, name="picked2_s%d" % a, align_bytes=64) for a in range(2)]
-        picked1 = [keep.tile([P, HALF], U32, name="picked1_%d" % h, align_bytes=64) for h in range(2)]
+        picked1 = keep.tile([P, J], U32, name="picked1", align_bytes=64)
         picked1_s = keep.tile([P, J], U8, name="picked1_s", align_bytes=64)
 
         def moving(kind, s):
             cols = slice(s * JS, (s + 1) * JS)
             if kind == "a":
-                half, c0 = divmod(s * JS, HALF)
-                return picked1[half][:, c0 : c0 + JS].bitcast(FP8X4), picked1_s[8:P, cols]
+                return picked1[:, cols].bitcast(FP8X4), picked1_s[8:P, cols]
             a = int(kind[1])
             return picked2[:, a * J + s * JS : a * J + (s + 1) * JS].bitcast(FP4X4), picked2_s[a][:, cols]
 
@@ -124,7 +123,7 @@ def tile_list_kg_absd_mix_gelu_kernel(
                     stop=(kind == "a" and t == PACK - 1),
                 )
 
-        h_codes = {(blk, hf): keep.tile([P, HALF], U32, name="hc_%d_%d" % (blk, hf), align_bytes=64) for blk in range(2) for hf in range(2)}
+        h_codes = {(1, hf): keep.tile([P, HALF], U32, name="hc_1_%d" % hf, align_bytes=64) for hf in range(2)}
         h_scales = {(blk, hf): keep.tile([P, HALF], U8, name="hs_%d_%d" % (blk, hf), align_bytes=64) for blk in range(2) for hf in range(2)}
 
         h_tiles = {}
@@ -135,11 +134,14 @@ def tile_list_kg_absd_mix_gelu_kernel(
             if i == 0:
                 h_tiles[blk, g] = keep.tile([P, group * JS * PACK], BF16, name="h_%d_%d" % (blk, g), align_bytes=64)
             h = h_tiles[blk, g]
-            nc.scalar.activation(
-                h[:, i * JS * PACK : (i + 1) * JS * PACK].rearrange("p (j t) -> p j t", t=PACK),
-                acc[blk, s][:].rearrange("p (t j) -> p j t", t=PACK),
-                ACT.Abs,
-            )
+            sums = acc[blk, s][:].rearrange("p (t j) -> p j t", t=PACK)
+            if blk == 1 and s % 4 == 3:
+                signed = ring.tile([P, JS * PACK], BF16, name="signed", align_bytes=64)
+                nc.vector.tensor_copy(signed[:].rearrange("p (j t) -> p j t", t=PACK), sums)
+                nc.vector.scalar_tensor_tensor(h[:], signed[:], -1.0, signed[:], ALU.mult, ALU.max)
+            else:
+                dst = h[:, i * JS * PACK : (i + 1) * JS * PACK]
+                nc.scalar.activation(dst.rearrange("p (j t) -> p j t", t=PACK), sums, ACT.Abs)
             if blk == 1:
                 quantise_h(blk, g)
 
@@ -162,15 +164,20 @@ def tile_list_kg_absd_mix_gelu_kernel(
                     rhs=h_codes[1, hf][:].bitcast(FP8X4), rhs_scale=h_scales[1, hf][:], start=False, stop=True,
                 )
                 res = ring.tile([P, HALF], F32, name="res", bufs=8)
-                nc.scalar.activation(res[:], y[:], ACT.Gelu_apprx_tanh, bias=bias[:, q : q + 1])
-                nc.sync.dma_start(out[cols, hf * HALF : (hf + 1) * HALF], res[:])
+                width = HALF // 2 if (hf, q) == (1, N // P - 1) else HALF
+                for c0 in range(0, HALF, width):
+                    part = slice(c0, c0 + width)
+                    nc.scalar.activation(res[:, part], y[:, part], ACT.Gelu_apprx_tanh, bias=bias[:, q : q + 1])
+                    nc.sync.dma_start(out[cols, hf * HALF + c0 : hf * HALF + c0 + width], res[:, part])
 
         nc.vector.memset(picked2_s[1][:].bitcast(I32), 0)
         nc.vector.tensor_copy(picked2_s[0][:], scales2[:].indirect(list2[:]))
-        nc.sync.dma_start(picked2_s[1][0:100, :].bitcast(I32), picked2_s[0][16:116, :].bitcast(I32))
+        for q in range(4):
+            nc.sync.dma_start(picked2_s[1][32 * q : 32 * q + 4, :].bitcast(I32), picked2_s[0][32 * q + 16 : 32 * q + 20, :].bitcast(I32))
         words1 = keep.tile([P, T], U32, name="words1", tag="scales2", align_bytes=64)
         load_words(words1, tab_words, 0, T)
         nc.vector.tensor_copy(pair2[:], words2[:].indirect(list2[:]))
+        load_piece("a", 0)
         nc.vector.tensor_copy(
             picked2[:].rearrange("p (d j) -> p d j", d=2), pair2[:].bitcast(U16).rearrange("p (j d) -> p d j", d=2)
         )
@@ -179,10 +186,13 @@ def tile_list_kg_absd_mix_gelu_kernel(
         quantise(("b0", 0), 0)
         cast(("b1", 0), "scalar", 0, 4)
         load_piece("b1", 1)
-        cast(("a", 0), "scalar", 0, 4)
-        load_piece("a", 1)
         quantise(("b1", 0), 0)
         nc.vector.tensor_copy(picked1_s[:], scales1[:].indirect(list1[:]))
+        nc.vector.tensor_copy(picked1[:], words1[:].indirect(list1[:]))
+        cast(("a", 0), "vector", 2, 4)
+        cast(("a", 0), "scalar", 0, 2)
+        load_piece("a", 1)
+        quantise(("a", 0), 2)
         quantise(("a", 0), 0)
         en = keep.tile([P, 8 * N], U8, name="en", tag="grp_a_0_0", align_bytes=64)
         en8, en4, en8_s, en4_s = en[:, 0 : 4 * N], en[:, 4 * N : 6 * N], en[:, 6 * N : 7 * N], en[:, 7 * N : 8 * N]
@@ -196,8 +206,6 @@ def tile_list_kg_absd_mix_gelu_kernel(
             stage1("b0", 0, s)
         for s in range(BANKS):
             stage1("b1", 0, s)
-        for hf in range(2):
-            nc.vector.tensor_copy(picked1[hf][:], words1[:].indirect(list1[:, hf * 32 : (hf + 1) * 32]))
         cast(("b0", 1), "vector", 0, 4)
         quantise(("b0", 1), 0)
         bias = keep.tile([P, N // P], F32, name="bias", tag="grp_b0_1_0", align_bytes=64)
@@ -213,6 +221,7 @@ def tile_list_kg_absd_mix_gelu_kernel(
         quantise(("a", 1), 2)
         quantise(("a", 1), 0)
         for hf in range(2):
+            h_codes[0, hf] = keep.tile([P, HALF], U32, name="hc_0_%d" % hf, tag="grp_a_1_%d" % (2 - 2 * hf), align_bytes=64)
             quantise_h(0, hf)
         for s in range(BANKS):
             stage1("b0", 1, s)

@@ -41,7 +41,7 @@ def tile_list_kg_absd_mix_gelu_kernel(
         warm = keep.tile([P, 2], F32, name="warm")
 
         nc.vector.memset(scales2[:].bitcast(I32), 0)
-        nc.gpsimd.memset(scales1[:].bitcast(I32), 0)
+        nc.vector.memset(scales1[:].bitcast(I32), 0)
         nc.vector.memset(warm[:, 0:1], 0.0)
         nc.scalar.activation(warm[:, 1:2], warm[:, 0:1], ACT.Gelu_apprx_tanh)
 
@@ -57,8 +57,8 @@ def tile_list_kg_absd_mix_gelu_kernel(
             nc.sync.dma_start(tile[:, c0:c1].bitcast(I32), rows[:, c0:c1])
 
         raw = {}
-        nc.sync.dma_start(list2[:], offs2)
         load_words(words2, tab2_words, 0, T // 2)
+        nc.sync.dma_start(list2[:], offs2)
         nc.sync.dma_start(list1[:], offs)
         for r in range(4):
             nc.sync.dma_start(scales2[r:P:16, :].bitcast(I32), tab2_scales[:, r:16:4, :].bitcast(I32).rearrange("a q t -> q a t"))
@@ -111,7 +111,8 @@ def tile_list_kg_absd_mix_gelu_kernel(
             if kind == "b0":
                 acc[blk, s] = psum.tile([P, PACK * JS], F32, name="acc", tag="bank%d" % s)
             rhs, rhs_s = moving(kind, s)
-            for t in range(PACK):
+            order = (2, 3, 0, 1) if kind == "a" else range(PACK)
+            for t in order:
                 cols = slice(t * P, (t + 1) * P)
                 nc.tensor.matmul_mx(
                     acc[blk, s][:, t * JS : (t + 1) * JS],
@@ -120,7 +121,7 @@ def tile_list_kg_absd_mix_gelu_kernel(
                     rhs=rhs,
                     rhs_scale=rhs_s,
                     start=(kind == "b0" and t == 0),
-                    stop=(kind == "a" and t == PACK - 1),
+                    stop=(kind == "a" and t == order[-1]),
                 )
 
         h_codes = {(1, hf): keep.tile([P, HALF], U32, name="hc_1_%d" % hf, align_bytes=64) for hf in range(2)}
@@ -172,8 +173,7 @@ def tile_list_kg_absd_mix_gelu_kernel(
 
         nc.vector.memset(picked2_s[1][:].bitcast(I32), 0)
         nc.vector.tensor_copy(picked2_s[0][:], scales2[:].indirect(list2[:]))
-        for q in range(4):
-            nc.sync.dma_start(picked2_s[1][32 * q : 32 * q + 4, :].bitcast(I32), picked2_s[0][32 * q + 16 : 32 * q + 20, :].bitcast(I32))
+        nc.sync.dma_start(picked2_s[1][0:100, :].bitcast(I32), picked2_s[0][16:116, :].bitcast(I32))
         words1 = keep.tile([P, T], U32, name="words1", tag="scales2", align_bytes=64)
         load_words(words1, tab_words, 0, T)
         nc.vector.tensor_copy(pair2[:], words2[:].indirect(list2[:]))

from contextlib import ExitStack

import concourse.mybir as mybir

K, L, R, N, T, J = 512, 1024, 1024, 512, 4096, 1024
FLOPS = 2 * J * (K * R + L * R + R * N)

F32 = mybir.dt.float32
BF16 = mybir.dt.bfloat16
I32 = mybir.dt.int32
U32 = mybir.dt.uint32
U16 = mybir.dt.uint16
U8 = mybir.dt.uint8
FP8X4 = mybir.dt.float8_e4m3fn_x4
FP4X4 = mybir.dt.float4_e2m1fn_x4
ACT = mybir.ActivationFunctionType
ALU = mybir.AluOpType

P = 128
PACK = 4
KP = P * PACK
JS = 128
BANKS = J // JS
HALF = J // 2


def tile_list_kg_absd_mix_gelu_kernel(
    tc, tab_words, tab_scales, tab2_words, tab2_scales, wa, wb, en8_words, en8_scales, en4_words, en4_scales, b, offs, offs2, out
):
    nc = tc.nc
    with ExitStack() as ctx:
        keep = ctx.enter_context(tc.tile_pool(name="keep", bufs=1))
        ring = ctx.enter_context(tc.tile_pool(name="ring", bufs=4))
        psum = ctx.enter_context(tc.psum_pool(name="psum", bufs=1))

        list1 = keep.tile([P, J // 16], U16, name="list1")
        list2 = keep.tile([P, J // 16], U16, name="list2")
        words2 = keep.tile([P, T], U32, name="words2", tag="words2", align_bytes=64)
        scales1 = keep.tile([P, T], U8, name="scales1", align_bytes=64)
        scales2 = keep.tile([P, T], U8, name="scales2", tag="scales2", align_bytes=64)
        warm = keep.tile([P, 2], F32, name="warm")

        nc.vector.memset(scales2[:].bitcast(I32), 0)
        nc.vector.memset(scales1[:].bitcast(I32), 0)
        nc.vector.memset(warm[:, 0:1], 0.0)
        nc.scalar.activation(warm[:, 1:2], warm[:, 0:1], ACT.Gelu_apprx_tanh)

        def load_piece(kind, blk):
            w, k0 = {"a": (wa, 0), "b0": (wb, 0), "b1": (wb, KP)}[kind]
            tag = "words2" if kind == "a" else "raw_" + kind
            raw[kind, blk] = keep.tile([P, PACK, KP], F32, name="raw_%s_%d" % (kind, blk), tag=tag, align_bytes=64)
            rows = w[k0 : k0 + KP, blk * KP : (blk + 1) * KP].rearrange("(p j) c -> p j c", j=PACK)
            nc.sync.dma_start(raw[kind, blk][:], rows)

        def load_words(tile, words, c0, c1):
            rows = words[0].rearrange("p t i -> p (t i)").bitcast(I32)
            nc.sync.dma_start(tile[:, c0:c1].bitcast(I32), rows[:, c0:c1])

        raw = {}
        load_words(words2, tab2_words, 0, T // 2)
        nc.sync.dma_start(list2[:], offs2)
        nc.sync.dma_start(list1[:], offs)
        for r in range(4):
            nc.sync.dma_start(scales2[r:P:16, :].bitcast(I32), tab2_scales[:, r:16:4, :].bitcast(I32).rearrange("a q t -> q a t"))
        load_words(words2, tab2_words, T // 2, T)
        load_piece("b0", 0)
        load_piece("b1", 0)
        for q in range(4):
            nc.sync.dma_start(scales1[32 * q + 8 : 32 * q + 12, :].bitcast(I32), tab_scales[0, 4 * q : 4 * q + 4, :].bitcast(I32))

        w_codes, w_scales, grouped = {}, {}, {}

        def cast(key, engine, t0, t1):
            sign = -1.0 if key[0] == "a" else 1.0
            name = "grp_%s_%d_%d" % (key[0], key[1], t0)
            g = keep.tile([P, (t1 - t0) * KP], BF16, name=name, tag=name, align_bytes=64)
            dst = g[:].rearrange("p (t m j) -> p m j t", j=PACK, m=P)
            src = raw[key][:].rearrange("p j (m t) -> p m j t", t=PACK)[:, :, :, t0:t1]
            if engine == "scalar":
                nc.scalar.activation(dst, src, ACT.Copy, scale=sign)
            elif sign < 0:
                nc.vector.tensor_scalar(dst, src, sign, None, ALU.mult)
            else:
                nc.vector.tensor_copy(dst, src)
            grouped[key, t0] = (g, t1)

        def quantise(key, t0):
            if key not in w_codes:
                w_codes[key] = keep.tile([P, KP], U32, name="wc_%s_%d" % key, align_bytes=64)
                w_scales[key] = keep.tile([P, KP], U8, name="ws_%s_%d" % key, align_bytes=64)
            g, t1 = grouped[key, t0]
            cols = slice(t0 * P, t1 * P)
            nc.vector.quantize_mx(w_codes[key][:, cols].bitcast(FP8X4), w_scales[key][:, cols], g[:])

        pair2 = keep.tile([P, J], U32, name="pair2", align_bytes=64)
        picked2 = keep.tile([P, 2 * J], U16, name="picked2", align_bytes=64)
        picked2_s = [keep.tile([P, J], U8, name="picked2_s%d" % a, align_bytes=64) for a in range(2)]
        picked1 = keep.tile([P, J], U32, name="picked1", align_bytes=64)
        picked1_s = keep.tile([P, J], U8, name="picked1_s", align_bytes=64)

        def moving(kind, s):
            cols = slice(s * JS, (s + 1) * JS)
            if kind == "a":
                return picked1[:, cols].bitcast(FP8X4), picked1_s[8:P, cols]
            a = int(kind[1])
            return picked2[:, a * J + s * JS : a * J + (s + 1) * JS].bitcast(FP4X4), picked2_s[a][:, cols]

        acc = {}

        def stage1(kind, blk, s):
            if kind == "b0":
                acc[blk, s] = psum.tile([P, PACK * JS], F32, name="acc", tag="bank%d" % s)
            rhs, rhs_s = moving(kind, s)
            order = (2, 3, 0, 1) if kind == "a" else range(PACK)
            for t in order:
                cols = slice(t * P, (t + 1) * P)
                nc.tensor.matmul_mx(
                    acc[blk, s][:, t * JS : (t + 1) * JS],
                    lhsT=w_codes[kind, blk][:, cols].bitcast(FP8X4),
                    lhsT_scale=w_scales[kind, blk][:, cols],
                    rhs=rhs,
                    rhs_scale=rhs_s,
                    start=(kind == "b0" and t == 0),
                    stop=(kind == "a" and t == order[-1]),
                )

        h_codes = {(1, hf): keep.tile([P, HALF], U32, name="hc_1_%d" % hf, align_bytes=64) for hf in range(2)}
        h_scales = {(blk, hf): keep.tile([P, HALF], U8, name="hs_%d_%d" % (blk, hf), align_bytes=64) for blk in range(2) for hf in range(2)}

        h_tiles = {}

        def join(blk, s):
            group = 4 if blk == 0 else 1
            g, i = divmod(s, group)
            if i == 0:
                h_tiles[blk, g] = keep.tile([P, group * JS * PACK], BF16, name="h_%d_%d" % (blk, g), align_bytes=64)
            h = h_tiles[blk, g]
            sums = acc[blk, s][:].rearrange("p (t j) -> p j t", t=PACK)
            if blk == 1 and s % 4 == 3:
                signed = ring.tile([P, JS * PACK], BF16, name="signed", align_bytes=64)
                nc.vector.tensor_copy(signed[:].rearrange("p (j t) -> p j t", t=PACK), sums)
                nc.vector.scalar_tensor_tensor(h[:], signed[:], -1.0, signed[:], ALU.mult, ALU.max)
            else:
                dst = h[:, i * JS * PACK : (i + 1) * JS * PACK]
                nc.scalar.activation(dst.rearrange("p (j t) -> p j t", t=PACK), sums, ACT.Abs)
            if blk == 1:
                quantise_h(blk, g)

        def quantise_h(blk, g):
            group = 4 if blk == 0 else 1
            hf, c0 = divmod(g * group * JS, HALF)
            cols = slice(c0, c0 + group * JS)
            nc.vector.quantize_mx(h_codes[blk, hf][:, cols].bitcast(FP8X4), h_scales[blk, hf][:, cols], h_tiles[blk, g][:])

        def stage2(hf):
            for q in range(N // P):
                y = psum.tile([P, HALF], F32, name="y", tag="bank%d" % (hf * 4 + q))
                cols = slice(q * P, (q + 1) * P)
                nc.tensor.matmul_mx(
                    y[:], lhsT=en8[:, 4 * q * P : 4 * (q + 1) * P].bitcast(FP8X4), lhsT_scale=en8_s[:, cols],
                    rhs=h_codes[0, hf][:].bitcast(FP8X4), rhs_scale=h_scales[0, hf][:], start=True, stop=False,
                )
                nc.tensor.matmul_mx(
                    y[:], lhsT=en4[:, 2 * q * P : 2 * (q + 1) * P].bitcast(FP4X4), lhsT_scale=en4_s[:, cols],
                    rhs=h_codes[1, hf][:].bitcast(FP8X4), rhs_scale=h_scales[1, hf][:], start=False, stop=True,
                )
                res = ring.tile([P, HALF], F32, name="res", bufs=8)
                width = HALF // 2 if (hf, q) == (1, N // P - 1) else HALF
                for c0 in range(0, HALF, width):
                    part = slice(c0, c0 + width)
                    nc.scalar.activation(res[:, part], y[:, part], ACT.Gelu_apprx_tanh, bias=bias[:, q : q + 1])
                    nc.sync.dma_start(out[cols, hf * HALF + c0 : hf * HALF + c0 + width], res[:, part])

        nc.vector.memset(picked2_s[1][:].bitcast(I32), 0)
        nc.vector.tensor_copy(picked2_s[0][:], scales2[:].indirect(list2[:]))
        nc.sync.dma_start(picked2_s[1][0:100, :].bitcast(I32), picked2_s[0][16:116, :].bitcast(I32))
        words1 = keep.tile([P, T], U32, name="words1", tag="scales2", align_bytes=64)
        load_words(words1, tab_words, 0, T)
        nc.vector.tensor_copy(pair2[:], words2[:].indirect(list2[:]))
        load_piece("a", 0)
        nc.vector.tensor_copy(
            picked2[:].rearrange("p (d j) -> p d j", d=2), pair2[:].bitcast(U16).rearrange("p (j d) -> p d j", d=2)
        )
        cast(("b0", 0), "scalar", 0, 4)
        load_piece("b0", 1)
        quantise(("b0", 0), 0)
        cast(("b1", 0), "scalar", 0, 4)
        load_piece("b1", 1)
        quantise(("b1", 0), 0)
        nc.vector.tensor_copy(picked1_s[:], scales1[:].indirect(list1[:]))
        nc.vector.tensor_copy(picked1[:], words1[:].indirect(list1[:]))
        cast(("a", 0), "vector", 2, 4)
        cast(("a", 0), "scalar", 0, 2)
        load_piece("a", 1)
        quantise(("a", 0), 2)
        quantise(("a", 0), 0)
        en = keep.tile([P, 8 * N], U8, name="en", tag="grp_a_0_0", align_bytes=64)
        en8, en4, en8_s, en4_s = en[:, 0 : 4 * N], en[:, 4 * N : 6 * N], en[:, 6 * N : 7 * N], en[:, 7 * N : 8 * N]
        nc.sync.dma_start(en8.bitcast(I32), en8_words[0].rearrange("p n i -> p (n i)").bitcast(I32))
        nc.sync.dma_start(en4.bitcast(I32), en4_words[0].bitcast(I32))
        nc.vector.memset(en[:, 6 * N : 8 * N].bitcast(I32), 0)
        for q in range(4):
            nc.sync.dma_start(en8_s[32 * q : 32 * q + 4, :].bitcast(I32), en8_scales[0, 4 * q : 4 * q + 4, :].bitcast(I32))
            nc.sync.dma_start(en4_s[32 * q : 32 * q + 4, :].bitcast(I32), en4_scales[0, 4 * q : 4 * q + 4, :].bitcast(I32))
        for s in range(BANKS):
            stage1("b0", 0, s)
        for s in range(BANKS):
            stage1("b1", 0, s)
        cast(("b0", 1), "vector", 0, 4)
        quantise(("b0", 1), 0)
        bias = keep.tile([P, N // P], F32, name="bias", tag="grp_b0_1_0", align_bytes=64)
        with nc.allow_non_contiguous_dma(reason="one bias value to a partition"):
            nc.sync.dma_start(bias[:], b.rearrange("(c p) -> p c", p=P))
        for s in range(BANKS):
            stage1("a", 0, s)
            join(0, s)
        cast(("b1", 1), "vector", 0, 4)
        quantise(("b1", 1), 0)
        cast(("a", 1), "vector", 2, 4)
        cast(("a", 1), "scalar", 0, 2)
        quantise(("a", 1), 2)
        quantise(("a", 1), 0)
        for hf in range(2):
            h_codes[0, hf] = keep.tile([P, HALF], U32, name="hc_0_%d" % hf, tag="grp_a_1_%d" % (2 - 2 * hf), align_bytes=64)
            quantise_h(0, hf)
        for s in range(BANKS):
            stage1("b0", 1, s)
        for s in range(4):
            stage1("b1", 1, s)
        for s in range(4):
            stage1("a", 1, s)
            join(1, s)
        for s in range(4, BANKS):
            stage1("b1", 1, s)
            stage1("a", 1, s)
            join(1, s)
        for hf in range(2):
            stage2(hf)
